import numpy as np
import ml_dtypes


def mxq(x, axis, fmt="e4m3"):
    dtype, down = {"e4m3": (ml_dtypes.float8_e4m3fn, 7), "e5m2": (ml_dtypes.float8_e5m2, 14)}[fmt]
    v = np.moveaxis(np.asarray(x, np.float32).astype(ml_dtypes.bfloat16).astype(np.float64), axis, -1)
    blocks = v.reshape(v.shape[:-1] + (-1, 32))
    amax = np.abs(blocks).max(-1, keepdims=True)
    byte = np.maximum(np.where(amax > 0, np.frexp(amax)[1] - 1 + 127, 0) - down, 1)
    scale = np.exp2(byte - 127.0)
    codes = (blocks / scale).astype(np.float32).astype(dtype).astype(np.float64)
    return np.moveaxis((codes * scale).reshape(v.shape), -1, axis)


WIDE = False


def mx_kscale(k):
    if not WIDE:
        return np.ones(k)
    levels = np.array([10, -10, 5, -5, 0])
    if k % 512:
        return np.exp2(np.random.permutation(np.resize(levels, k // 32))).repeat(32)
    a = np.empty((k // 512, 16))
    for p in range(k // 512):
        a[p, :8] = np.random.permutation(np.resize(levels, 8))
        for g in range(8):
            far = levels[np.abs(levels - a[p, g]) >= 10]
            a[p, g + 8] = far[np.random.randint(len(far))]
    return np.exp2(a.ravel()).repeat(32)


def f64(x):
    return np.asarray(x).astype(np.float64)


def striped(idx):
    return np.tile(idx.reshape(-1, 16).T, (8, 1)).astype(np.uint16)


def unstriped(offs):
    return offs[:16].T.reshape(-1).astype(np.int64)


E2M1 = np.array([0.0, 0.5, 1.0, 1.5, 2.0, 3.0, 4.0, 6.0, -0.0, -0.5, -1.0, -1.5, -2.0, -3.0, -4.0, -6.0])


def pack_weight(w, fmt):
    k, n = w.shape
    w = f64(np.asarray(w, np.float32).astype(ml_dtypes.bfloat16)).reshape(k // 32, 32, n)
    amax = np.abs(w).max(1)
    if fmt == "e4m3":
        byte = np.frexp(amax)[1] - 1 + 127 - 7
    else:
        mant, ex = np.frexp(amax / 6.0)
        byte = np.where(mant > 0.5, ex, ex - 1) + 127
    byte = np.clip(np.where(amax > 0, byte, 1), 1, 254)
    scaled = (w * np.exp2(127.0 - byte)[:, None, :]).reshape(k, n).astype(np.float32)
    by_word = np.ascontiguousarray(scaled.reshape(k // 512, 128, 4, n).transpose(0, 1, 3, 2))
    if fmt == "e4m3":
        words = by_word.astype(ml_dtypes.float8_e4m3fn).view(np.uint8)
    else:
        c = by_word.astype(ml_dtypes.float4_e2m1fn).view(np.uint8) & 0xF
        words = (c[..., 0::2] | (c[..., 1::2] << 4)).reshape(k // 512, 128, 2 * n)
    return np.ascontiguousarray(words), np.ascontiguousarray(byte.astype(np.uint8).reshape(k // 512, 16, n))


def unpack_weight(words, scales, fmt):
    g, _, n = scales.shape
    words = np.ascontiguousarray(words).reshape(g, 128, n, -1)
    if fmt == "e4m3":
        vals = words.view(ml_dtypes.float8_e4m3fn).astype(np.float64)
    else:
        nib = np.empty((g, 128, n, 4), np.uint8)
        nib[..., 0::2] = words & 0xF
        nib[..., 1::2] = words >> 4
        vals = E2M1[nib]
    vals = vals * np.repeat(np.exp2(scales.astype(np.float64) - 127.0), 8, axis=1)[..., None]
    return vals.transpose(0, 1, 3, 2).reshape(g * 512, n)


def gelu(v):
    return 0.5 * v * (1.0 + np.tanh(np.sqrt(2.0 / np.pi) * (v + 0.044715 * v**3)))


K, T, S, H, P, N = 1536, 2048, 1024, 512, 512, 384

def setup_inputs():
    n = np.random.standard_normal
    s = mx_kscale(K)[:, None]
    u = mx_kscale(H)[:, None]
    d = {}
    d["tab_words"], d["tab_scales"] = pack_weight(n((K, T)) * s, "e2m1")
    d["offs"] = striped(np.random.permutation(T)[:S])
    d["pos1"] = striped(np.random.permutation(S)[:P])
    d["pos2"] = striped(np.random.permutation(S)[:P])
    d["w1"] = (1.3 * n((K, H)) / K ** 0.5 / s).astype(np.float32)
    d["b1"] = (0.6 * n(H)).astype(np.float32)
    d["gain"] = (np.exp(0.3 * n(H)) * u[:, 0]).astype(np.float32)
    d["w2_words"], d["w2_scales"] = pack_weight(1.8 * n((H, H)) / H ** 0.5 / u, "e4m3")
    d["tone"] = (np.exp(0.3 * n(H)) * u[:, 0]).astype(np.float32)
    d["w3_words"], d["w3_scales"] = pack_weight(n((H, N)) / H ** 0.5 / u, "e2m1")
    return d

def reference(tab_words, tab_scales, offs, pos1, pos2, w1, b1, gain, w2_words, w2_scales, tone, w3_words, w3_scales):
    v = unpack_weight(tab_words, tab_scales, "e2m1")[:, unstriped(offs)]
    h = (mxq(f64(w1), 0, "e4m3").T @ v) + f64(b1)[:, None]
    x = np.tanh(h) * f64(gain)[:, None]
    w2 = unpack_weight(w2_words, w2_scales, "e4m3")
    f1 = w2.T @ mxq(x[:, unstriped(pos1)], 0, "e4m3")
    f2 = w2.T @ mxq(x[:, unstriped(pos2)], 0, "e4m3")
    e1 = h[:, unstriped(pos2)] - f1
    e2 = h[:, unstriped(pos1)] - f2
    z = np.maximum(e1, e2) * f64(tone)[:, None]
    w3 = unpack_weight(w3_words, w3_scales, "e2m1")
    return w3.T @ mxq(z, 0, "e4m3")

@@ -1,0 +1,291 @@
+from contextlib import ExitStack
+
+import concourse.mybir as mybir
+
+K, T, S, H, NP, N = 1536, 2048, 1024, 512, 512, 384
+FLOPS = 2 * (K * H * S + 2 * H * H * NP + H * N * NP)
+
+F32 = mybir.dt.float32
+BF16 = mybir.dt.bfloat16
+I32 = mybir.dt.int32
+U16 = mybir.dt.uint16
+U8 = mybir.dt.uint8
+FP8X4 = mybir.dt.float8_e4m3fn_x4
+FP4X4 = mybir.dt.float4_e2m1fn_x4
+ALU = mybir.AluOpType
+ACT = mybir.ActivationFunctionType
+
+P = 128
+PACK = 4
+PASSES = K // (P * PACK)
+BANK = 512
+FIRST_ROW = 32 - 4 * PASSES
+CHUNKS = [128,128,128,128]
+X_MODE = []
+Z_MODE = ["S","S","V","V"]
+LAST_PIECES = 2
+
+
+def tile_list_hank_pair_features_kernel(
+    tc, tab_words, tab_scales, offs, pos1, pos2, w1, b1, gain, w2_words, w2_scales, tone, w3_words, w3_scales, out
+):
+    nc = tc.nc
+    with ExitStack() as ctx:
+        keep = ctx.enter_context(tc.tile_pool(name="keep", bufs=1))
+        psum = ctx.enter_context(tc.psum_pool(name="psum", bufs=8))
+
+        def sbuf(name, shape, dtype):
+            return keep.tile(shape, dtype, name=name, align_bytes=64)
+
+        def bank(name):
+            return psum.tile([P, BANK], F32, name=name, tag="bank")
+
+        offs_sb = sbuf("offs_sb", [P, S // 16], U16)
+        pos_sb = [sbuf("pos%d_sb" % s, [P, NP // 16], U16) for s in range(2)]
+        tabw = [sbuf("tabw%d" % a, [P, T], U16) for a in range(PASSES)]
+        tabs = sbuf("tabs", [P, T], U8)
+        moved = sbuf("moved", [P, PASSES * S], U8)
+        ws2 = sbuf("ws2", [P, H], U8)
+        ws3 = sbuf("ws3", [P, N], U8)
+        warm = sbuf("warm", [P, 1], F32)
+        warm2 = sbuf("warm2", [P, 1], F32)
+
+        for q in range(4):
+            nc.vector.memset(tabs[32 * q : 32 * q + FIRST_ROW, :].bitcast(I32), 0)
+        nc.vector.memset(warm[:], 0.0)
+        nc.scalar.activation(out=warm2[:], in_=warm[:], func=ACT.Tanh)
+        nc.gpsimd.memset(ws2[:].bitcast(I32), 0)
+        nc.gpsimd.memset(ws3[:].bitcast(I32), 0)
+        nc.gpsimd.memset(moved[:].bitcast(I32), 0)
+
+        def w1_rows(a):
+            return w1[a * P * PACK : (a + 1) * P * PACK, :].rearrange("(p j) c -> p j c", j=PACK)
+
+        pieces = [1] * (PASSES - 1) + [LAST_PIECES]
+        w1_raw = [
+            [sbuf("w1_raw%d_%d" % (a, u), [P, PACK, H // pieces[a]], F32) for u in range(pieces[a])]
+            for a in range(PASSES)
+        ]
+
+        b1_sb = sbuf("b1_sb", [P, PACK], F32)
+        gain_sb = sbuf("gain_sb", [P, PACK], F32)
+        tone_sb = sbuf("tone_sb", [P, PACK], F32)
+        nc.sync.dma_start(out=offs_sb[:], in_=offs)
+        for q in range(4):
+            nc.sync.dma_start(
+                out=tabs[32 * q + FIRST_ROW : 32 * (q + 1), :].bitcast(I32),
+                in_=tab_scales[:, 4 * q : 4 * q + 4, :].bitcast(I32),
+            )
+        nc.sync.dma_start(out=tabw[0][:].bitcast(I32), in_=tab_words[0].bitcast(I32))
+        for a in range(PASSES):
+            width = H // pieces[a]
+            for u in range(pieces[a]):
+                nc.sync.dma_start(out=w1_raw[a][u][:], in_=w1_rows(a)[:, :, u * width : (u + 1) * width])
+            if a + 1 < PASSES:
+                nc.sync.dma_start(out=tabw[a + 1][:].bitcast(I32), in_=tab_words[a + 1].bitcast(I32))
+            if a == 0:
+                nc.sync.dma_start(out=b1_sb[:], in_=b1.rearrange("(p t) -> p t", t=PACK))
+                nc.sync.dma_start(out=pos_sb[0][:], in_=pos1)
+                nc.sync.dma_start(out=pos_sb[1][:], in_=pos2)
+                nc.sync.dma_start(out=gain_sb[:], in_=gain.rearrange("(p t) -> p t", t=PACK))
+                nc.sync.dma_start(out=tone_sb[:], in_=tone.rearrange("(p t) -> p t", t=PACK))
+        w2_raw = sbuf("w2_raw", [P, H], I32)
+        w3_sb = sbuf("w3_sb", [P, 2 * N], U8)
+        nc.sync.dma_start(out=w2_raw[:], in_=w2_words[0].rearrange("p c i -> p (c i)").bitcast(I32))
+        for q in range(4):
+            nc.sync.dma_start(
+                out=ws2[32 * q : 32 * q + 4, :].bitcast(I32), in_=w2_scales[0, 4 * q : 4 * q + 4, :].bitcast(I32)
+            )
+        nc.sync.dma_start(out=w3_sb[:].bitcast(I32), in_=w3_words[0].bitcast(I32))
+        for q in range(4):
+            nc.sync.dma_start(
+                out=ws3[32 * q : 32 * q + 4, :].bitcast(I32), in_=w3_scales[0, 4 * q : 4 * q + 4, :].bitcast(I32)
+            )
+
+        picked_scales = sbuf("picked_scales", [P, S], U8)
+        picked_words = [[sbuf("pw%d_%d" % (a, v), [P, BANK], U16) for v in range(2)] for a in range(PASSES)]
+
+        def gather_words(a):
+            for v in range(2):
+                nc.vector.tensor_copy(
+                    out=picked_words[a][v][:], in_=tabw[a][:].indirect(offs_sb[:, 32 * v : 32 * (v + 1)])
+                )
+
+        nc.vector.tensor_copy(out=picked_scales[:], in_=tabs[:].indirect(offs_sb[:]))
+        gather_words(0)
+        live = 3 * 32 + 4
+        for a in range(PASSES):
+            nc.gpsimd.dma_start(
+                out=moved[0:live, a * S : (a + 1) * S].bitcast(I32),
+                in_=picked_scales[FIRST_ROW + 4 * a : FIRST_ROW + 4 * a + live, :].bitcast(I32),
+            )
+
+        def table_scales(a, v):
+            return moved[:, a * S + v * BANK : a * S + (v + 1) * BANK]
+
+        h_banks = [[bank("h_bank%d_%d" % (t, v)) for v in range(2)] for t in range(PACK)]
+        w1_q = []
+        for a in range(PASSES):
+            grouped = sbuf("w1_grouped%d" % a, [P, PACK * H], BF16)
+            by_m = grouped[:].rearrange("p (t m j) -> p m j t", t=PACK, j=PACK)
+            m_width = P // pieces[a]
+            for u in range(pieces[a]):
+                nc.scalar.copy(
+                    out=by_m[:, u * m_width : (u + 1) * m_width, :, :],
+                    in_=w1_raw[a][u][:].rearrange("p j (m t) -> p m j t", t=PACK),
+                )
+            if a > 0:
+                gather_words(a)
+            codes = sbuf("w1_codes%d" % a, [P, H], I32)
+            scales = sbuf("w1_scales%d" % a, [P, H], U8)
+            nc.vector.quantize_mx(out=codes[:].bitcast(FP8X4), scales=scales[:], in_=grouped[:])
+            w1_q.append((codes, scales))
+        for t in range(PACK):
+            for a in range(PASSES):
+                codes, scales = w1_q[a]
+                for v in range(2):
+                    nc.tensor.matmul_mx(
+                        out=h_banks[t][v][:],
+                        lhsT=codes[:, t * P : (t + 1) * P].bitcast(FP8X4),
+                        lhsT_scale=scales[:, t * P : (t + 1) * P],
+                        rhs=picked_words[a][v][:].bitcast(FP4X4),
+                        rhs_scale=table_scales(a, v),
+                        start=(a == 0),
+                        stop=(a == PASSES - 1),
+                    )
+
+        w2_codes = sbuf("w2_codes", [P, H], I32)
+        w2_sc = sbuf("w2_sc", [P, H], U8)
+        nc.vector.tensor_copy(
+            out=w2_codes[:].rearrange("p (t m) -> p t m", t=PACK), in_=w2_raw[:].rearrange("p (m t) -> p t m", t=PACK)
+        )
+        nc.vector.tensor_copy(
+            out=w2_sc[:].rearrange("p (t m) -> p t m", t=PACK), in_=ws2[:].rearrange("p (m t) -> p t m", t=PACK)
+        )
+
+        h = [sbuf("h%d" % t, [P, S], F32) for t in range(PACK)]
+        for t in range(PACK):
+            for v in range(2):
+                cols = slice(v * BANK, (v + 1) * BANK)
+                if t == 0 and v == 1:
+                    nc.vector.tensor_scalar(
+                        out=h[t][:, cols], in0=h_banks[t][v][:], scalar1=b1_sb[:, t : t + 1], scalar2=None, op0=ALU.add
+                    )
+                else:
+                    nc.scalar.activation(
+                        out=h[t][:, cols], in_=h_banks[t][v][:], func=ACT.Identity, bias=b1_sb[:, t : t + 1]
+                    )
+
+        def planes(ap, width):
+            return ap.rearrange("p t (c i) -> p c t i", i=4)
+
+        def woven(ap):
+            return ap.rearrange("p (c i t) -> p c t i", t=PACK, i=4)
+
+        def spread(vec, width):
+            return vec[:].rearrange("p (a t b) -> p a t b", a=1, b=1).to_broadcast([P, width // 4, PACK, 4])
+
+        def scale_round_weave(mode, name, src, vec, width):
+            dst = sbuf(name + "_bf", [P, PACK * width], BF16)
+            if mode == "V":
+                nc.vector.tensor_tensor(out=woven(dst[:]), in0=planes(src, width), in1=spread(vec, width), op=ALU.mult)
+            else:
+                flat = sbuf(name + "_flat", [P, PACK, width], BF16)
+                for t in range(PACK):
+                    nc.scalar.activation(out=flat[:, t, :], in_=src[:, t, :], func=ACT.Copy, scale=vec[:, t : t + 1])
+                if mode == "S":
+                    nc.scalar.copy(out=woven(dst[:]), in_=planes(flat[:], width))
+                else:
+                    nc.vector.tensor_copy(out=woven(dst[:]), in_=planes(flat[:], width))
+            return dst
+
+        def quantize(name, src, width):
+            codes = sbuf(name + "_codes", [P, width], I32)
+            scales = sbuf(name + "_scales", [P, width], U8)
+            nc.vector.quantize_mx(out=codes[:].bitcast(FP8X4), scales=scales[:], in_=src[:])
+            return codes, scales
+
+        starts = [sum(CHUNKS[:c]) for c in range(len(CHUNKS))]
+        hg = [sbuf("hg%d" % s, [P, PACK, NP], F32) for s in range(2)]
+        th = [sbuf("th%d" % s, [P, PACK, NP], F32) for s in range(2)]
+        for t in range(PACK):
+            for s in range(2):
+                nc.vector.tensor_copy(out=hg[s][:, t, :], in_=h[t][:].indirect(pos_sb[s][:]))
+        head = 128
+        x_flat = [sbuf("x_flat%d" % s, [P, PACK, NP - head], BF16) for s in range(2)]
+
+        def apply_gain(s, t):
+            nc.scalar.activation(
+                out=x_flat[s][:, t, :], in_=th[s][:, t, head:], func=ACT.Copy, scale=gain_sb[:, t : t + 1]
+            )
+
+        early = 2
+        for t in range(PACK):
+            for s in range(2):
+                nc.scalar.activation(out=th[s][:, t, :], in_=hg[s][:, t, :], func=ACT.Tanh)
+                if t < early:
+                    apply_gain(s, t)
+        xb = {}
+        for c, width in enumerate(CHUNKS):
+            for s in range(2):
+                cols = slice(starts[c], starts[c] + width)
+                if starts[c] < head:
+                    xb[c, s] = scale_round_weave("V", "x%d_%d" % (c, s), th[s][:, :, cols], gain_sb, width)
+                    continue
+                if starts[c] == head:
+                    for t in range(early, PACK):
+                        apply_gain(s, t)
+                xb[c, s] = sbuf("x%d_%d_bf" % (c, s), [P, PACK * width], BF16)
+                nc.scalar.copy(
+                    out=woven(xb[c, s][:]), in_=planes(x_flat[s][:, :, starts[c] - head : starts[c] - head + width], width)
+                )
+
+        out_rows = out.rearrange("(g p) j -> p g j", p=P)
+        for c, width in enumerate(CHUNKS):
+            per_bank = BANK // width
+            diff = []
+            for s in range(2):
+                codes, scales = quantize("xq%d_%d" % (c, s), xb[c, s], width)
+                e = sbuf("e%d_%d" % (c, s), [P, PACK, width], F32)
+                for t0 in range(0, PACK, per_bank):
+                    f = bank("f%d_%d_%d" % (c, s, t0))
+                    for t in range(t0, t0 + per_bank):
+                        nc.tensor.matmul_mx(
+                            out=f[:, (t - t0) * width : (t - t0 + 1) * width],
+                            lhsT=w2_codes[:, t * P : (t + 1) * P].bitcast(FP8X4),
+                            lhsT_scale=w2_sc[:, t * P : (t + 1) * P],
+                            rhs=codes[:].bitcast(FP8X4),
+                            rhs_scale=scales[:],
+                            start=True,
+                            stop=True,
+                        )
+                    nc.vector.tensor_tensor(
+                        out=e[:, t0 : t0 + per_bank, :],
+                        in0=hg[1 - s][:, t0 : t0 + per_bank, starts[c] : starts[c] + width],
+                        in1=f[:].rearrange("p (t j) -> p t j", j=width),
+                        op=ALU.subtract,
+                    )
+                diff.append(e)
+            larger = sbuf("larger%d" % c, [P, PACK, width], F32)
+            nc.vector.tensor_tensor(out=larger[:], in0=diff[0][:], in1=diff[1][:], op=ALU.max)
+            zb = scale_round_weave(Z_MODE[c], "z%d" % c, larger[:], tone_sb, width)
+            codes, scales = quantize("zq%d" % c, zb, width)
+            staged = sbuf("staged%d" % c, [P, N // P, width], F32)
+            for g0 in range(0, N // P, per_bank):
+                count = min(per_bank, N // P - g0)
+                acc = bank("acc%d_%d" % (c, g0))
+                for g in range(g0, g0 + count):
+                    nc.tensor.matmul_mx(
+                        out=acc[:, (g - g0) * width : (g - g0 + 1) * width],
+                        lhsT=w3_sb[:, 2 * g * P : 2 * (g + 1) * P].bitcast(FP4X4),
+                        lhsT_scale=ws3[:, g * P : (g + 1) * P],
+                        rhs=codes[:].bitcast(FP8X4),
+                        rhs_scale=scales[:],
+                        start=True,
+                        stop=True,
+                    )
+                nc.scalar.copy(
+                    out=staged[:, g0 : g0 + count, :],
+                    in_=acc[:, 0 : count * width].rearrange("p (g j) -> p g j", j=width),
+                )
+            nc.sync.dma_start(out=out_rows[:, :, starts[c] : starts[c] + width], in_=staged[:])

@@ -22,7 +22,7 @@ BANK = 512
 FIRST_ROW = 32 - 4 * PASSES
 CHUNKS = [128,128,128,128]
 X_MODE = []
-Z_MODE = ["S","S","V","V"]
+Z_MODE = ["V","V","V","V"]
 LAST_PIECES = 2
 
 
@@ -50,10 +50,10 @@ def tile_list_hank_pair_features_kernel(
         warm = sbuf("warm", [P, 1], F32)
         warm2 = sbuf("warm2", [P, 1], F32)
 
-        for q in range(4):
-            nc.vector.memset(tabs[32 * q : 32 * q + FIRST_ROW, :].bitcast(I32), 0)
         nc.vector.memset(warm[:], 0.0)
         nc.scalar.activation(out=warm2[:], in_=warm[:], func=ACT.Tanh)
+        for q in range(4):
+            nc.vector.memset(tabs[32 * q : 32 * q + FIRST_ROW, :].bitcast(I32), 0)
         nc.gpsimd.memset(ws2[:].bitcast(I32), 0)
         nc.gpsimd.memset(ws3[:].bitcast(I32), 0)
         nc.gpsimd.memset(moved[:].bitcast(I32), 0)
@@ -61,7 +61,7 @@ def tile_list_hank_pair_features_kernel(
         def w1_rows(a):
             return w1[a * P * PACK : (a + 1) * P * PACK, :].rearrange("(p j) c -> p j c", j=PACK)
 
-        pieces = [1] * (PASSES - 1) + [LAST_PIECES]
+        pieces = [1,2,2]
         w1_raw = [
             [sbuf("w1_raw%d_%d" % (a, u), [P, PACK, H // pieces[a]], F32) for u in range(pieces[a])]
             for a in range(PASSES)
@@ -71,36 +71,35 @@ def tile_list_hank_pair_features_kernel(
         gain_sb = sbuf("gain_sb", [P, PACK], F32)
         tone_sb = sbuf("tone_sb", [P, PACK], F32)
         nc.sync.dma_start(out=offs_sb[:], in_=offs)
-        for q in range(4):
-            nc.sync.dma_start(
-                out=tabs[32 * q + FIRST_ROW : 32 * (q + 1), :].bitcast(I32),
-                in_=tab_scales[:, 4 * q : 4 * q + 4, :].bitcast(I32),
-            )
-        nc.sync.dma_start(out=tabw[0][:].bitcast(I32), in_=tab_words[0].bitcast(I32))
-        for a in range(PASSES):
+
+        def load_table(a):
+            nc.sync.dma_start(out=tabw[a][:].bitcast(I32), in_=tab_words[a].bitcast(I32))
+
+        def load_w1(a, u):
             width = H // pieces[a]
-            for u in range(pieces[a]):
-                nc.sync.dma_start(out=w1_raw[a][u][:], in_=w1_rows(a)[:, :, u * width : (u + 1) * width])
-            if a + 1 < PASSES:
-                nc.sync.dma_start(out=tabw[a + 1][:].bitcast(I32), in_=tab_words[a + 1].bitcast(I32))
-            if a == 0:
-                nc.sync.dma_start(out=b1_sb[:], in_=b1.rearrange("(p t) -> p t", t=PACK))
-                nc.sync.dma_start(out=pos_sb[0][:], in_=pos1)
-                nc.sync.dma_start(out=pos_sb[1][:], in_=pos2)
-                nc.sync.dma_start(out=gain_sb[:], in_=gain.rearrange("(p t) -> p t", t=PACK))
-                nc.sync.dma_start(out=tone_sb[:], in_=tone.rearrange("(p t) -> p t", t=PACK))
+            nc.sync.dma_start(out=w1_raw[a][u][:], in_=w1_rows(a)[:, :, u * width : (u + 1) * width])
+
+        def load_table_scales():
+            for q in range(4):
+                nc.sync.dma_start(
+                    out=tabs[32 * q + FIRST_ROW : 32 * (q + 1), :].bitcast(I32),
+                    in_=tab_scales[:, 4 * q : 4 * q + 4, :].bitcast(I32),
+                )
+
+        load_table(0)
+        load_w1(0, 0)
+        load_table_scales()
+        load_w1(1, 0)
+        load_table(1)
+        load_w1(1, 1)
+        load_w1(2, 0)
+        load_table(2)
+        load_w1(2, 1)
         w2_raw = sbuf("w2_raw", [P, H], I32)
         w3_sb = sbuf("w3_sb", [P, 2 * N], U8)
-        nc.sync.dma_start(out=w2_raw[:], in_=w2_words[0].rearrange("p c i -> p (c i)").bitcast(I32))
-        for q in range(4):
-            nc.sync.dma_start(
-                out=ws2[32 * q : 32 * q + 4, :].bitcast(I32), in_=w2_scales[0, 4 * q : 4 * q + 4, :].bitcast(I32)
-            )
-        nc.sync.dma_start(out=w3_sb[:].bitcast(I32), in_=w3_words[0].bitcast(I32))
-        for q in range(4):
-            nc.sync.dma_start(
-                out=ws3[32 * q : 32 * q + 4, :].bitcast(I32), in_=w3_scales[0, 4 * q : 4 * q + 4, :].bitcast(I32)
-            )
+        nc.sync.dma_start(out=b1_sb[:], in_=b1.rearrange("(p t) -> p t", t=PACK))
+        nc.sync.dma_start(out=pos_sb[0][:], in_=pos1)
+        nc.sync.dma_start(out=pos_sb[1][:], in_=pos2)
 
         picked_scales = sbuf("picked_scales", [P, S], U8)
         picked_words = [[sbuf("pw%d_%d" % (a, v), [P, BANK], U16) for v in range(2)] for a in range(PASSES)]
@@ -111,14 +110,27 @@ def tile_list_hank_pair_features_kernel(
                     out=picked_words[a][v][:], in_=tabw[a][:].indirect(offs_sb[:, 32 * v : 32 * (v + 1)])
                 )
 
-        nc.vector.tensor_copy(out=picked_scales[:], in_=tabs[:].indirect(offs_sb[:]))
         gather_words(0)
+        nc.vector.tensor_copy(out=picked_scales[:], in_=tabs[:].indirect(offs_sb[:]))
         live = 3 * 32 + 4
         for a in range(PASSES):
-            nc.gpsimd.dma_start(
+            nc.sync.dma_start(
                 out=moved[0:live, a * S : (a + 1) * S].bitcast(I32),
                 in_=picked_scales[FIRST_ROW + 4 * a : FIRST_ROW + 4 * a + live, :].bitcast(I32),
             )
+        nc.sync.dma_start(out=w2_raw[:], in_=w2_words[0].rearrange("p c i -> p (c i)").bitcast(I32))
+        nc.sync.dma_start(out=gain_sb[:], in_=gain.rearrange("(p t) -> p t", t=PACK))
+        for q in range(4):
+            nc.sync.dma_start(
+                out=ws2[32 * q : 32 * q + 4, :].bitcast(I32), in_=w2_scales[0, 4 * q : 4 * q + 4, :].bitcast(I32)
+            )
+        nc.sync.dma_start(out=tone_sb[:], in_=tone.rearrange("(p t) -> p t", t=PACK))
+        nc.sync.dma_start(out=w3_sb[:].bitcast(I32), in_=w3_words[0].bitcast(I32))
+        for q in range(4):
+            nc.sync.dma_start(
+                out=ws3[32 * q : 32 * q + 4, :].bitcast(I32), in_=w3_scales[0, 4 * q : 4 * q + 4, :].bitcast(I32)
+            )
+
 
         def table_scales(a, v):
             return moved[:, a * S + v * BANK : a * S + (v + 1) * BANK]
@@ -138,7 +150,13 @@ def tile_list_hank_pair_features_kernel(
                 gather_words(a)
             codes = sbuf("w1_codes%d" % a, [P, H], I32)
             scales = sbuf("w1_scales%d" % a, [P, H], U8)
-            nc.vector.quantize_mx(out=codes[:].bitcast(FP8X4), scales=scales[:], in_=grouped[:])
+            cuts = [0, P, H] if a == PASSES - 1 else [0, H]
+            if a == PASSES - 1:
+                cuts = [0, P, 2 * P, H]
+            for lo, hi in zip(cuts, cuts[1:]):
+                nc.vector.quantize_mx(
+                    out=codes[:, lo:hi].bitcast(FP8X4), scales=scales[:, lo:hi], in_=grouped[:, PACK * lo : PACK * hi]
+                )
             w1_q.append((codes, scales))
         for t in range(PACK):
             for a in range(PASSES):
@@ -211,7 +229,7 @@ def tile_list_hank_pair_features_kernel(
         for t in range(PACK):
             for s in range(2):
                 nc.vector.tensor_copy(out=hg[s][:, t, :], in_=h[t][:].indirect(pos_sb[s][:]))
-        head = 128
+        head = 256
         x_flat = [sbuf("x_flat%d" % s, [P, PACK, NP - head], BF16) for s in range(2)]
 
         def apply_gain(s, t):
@@ -219,7 +237,7 @@ def tile_list_hank_pair_features_kernel(
                 out=x_flat[s][:, t, :], in_=th[s][:, t, head:], func=ACT.Copy, scale=gain_sb[:, t : t + 1]
             )
 
-        early = 2
+        early = 0
         for t in range(PACK):
             for s in range(2):
                 nc.scalar.activation(out=th[s][:, t, :], in_=hg[s][:, t, :], func=ACT.Tanh)
@@ -240,6 +258,7 @@ def tile_list_hank_pair_features_kernel(
                     out=woven(xb[c, s][:]), in_=planes(x_flat[s][:, :, starts[c] - head : starts[c] - head + width], width)
                 )
 
+        largers = []
         out_rows = out.rearrange("(g p) j -> p g j", p=P)
         for c, width in enumerate(CHUNKS):
             per_bank = BANK // width
@@ -268,6 +287,10 @@ def tile_list_hank_pair_features_kernel(
                 diff.append(e)
             larger = sbuf("larger%d" % c, [P, PACK, width], F32)
             nc.vector.tensor_tensor(out=larger[:], in0=diff[0][:], in1=diff[1][:], op=ALU.max)
+            largers.append(larger)
+        for c, width in enumerate(CHUNKS):
+            per_bank = BANK // width
+            larger = largers[c]
             zb = scale_round_weave(Z_MODE[c], "z%d" % c, larger[:], tone_sb, width)
             codes, scales = quantize("zq%d" % c, zb, width)
             staged = sbuf("staged%d" % c, [P, N // P, width], F32)

@@ -22,7 +22,7 @@ BANK = 512
 FIRST_ROW = 32 - 4 * PASSES
 CHUNKS = [128,128,128,128]
 X_MODE = []
-Z_MODE = ["V","V","V","V"]
+Z_MODE = ["S","S","V","V"]
 LAST_PIECES = 2
 
 
@@ -226,23 +226,25 @@ def tile_list_hank_pair_features_kernel(
         starts = [sum(CHUNKS[:c]) for c in range(len(CHUNKS))]
         hg = [sbuf("hg%d" % s, [P, PACK, NP], F32) for s in range(2)]
         th = [sbuf("th%d" % s, [P, PACK, NP], F32) for s in range(2)]
-        for t in range(PACK):
-            for s in range(2):
-                nc.vector.tensor_copy(out=hg[s][:, t, :], in_=h[t][:].indirect(pos_sb[s][:]))
-        head = 256
+        head = 128
+        early = PACK
         x_flat = [sbuf("x_flat%d" % s, [P, PACK, NP - head], BF16) for s in range(2)]
-
-        def apply_gain(s, t):
-            nc.scalar.activation(
-                out=x_flat[s][:, t, :], in_=th[s][:, t, head:], func=ACT.Copy, scale=gain_sb[:, t : t + 1]
-            )
-
-        early = 0
-        for t in range(PACK):
+        spans = [(t, 0, NP) for t in range(PACK - 1)] + [(PACK - 1, 0, head), (PACK - 1, head, NP)]
+        for t, lo, hi in spans:
             for s in range(2):
-                nc.scalar.activation(out=th[s][:, t, :], in_=hg[s][:, t, :], func=ACT.Tanh)
-                if t < early:
-                    apply_gain(s, t)
+                nc.vector.tensor_copy(out=hg[s][:, t, lo:hi], in_=h[t][:].indirect(pos_sb[s][:, lo // 16 : hi // 16]))
+        for t, lo, hi in spans:
+            for s in range(2):
+                nc.scalar.activation(out=th[s][:, t, lo:hi], in_=hg[s][:, t, lo:hi], func=ACT.Tanh)
+                if hi > head:
+                    nc.gpsimd.tensor_scalar(
+                        out=x_flat[s][:, t, :],
+                        in0=th[s][:, t, head:],
+                        scalar1=gain_sb[:, t : t + 1],
+                        scalar2=0.0,
+                        op0=ALU.mult,
+                        op1=ALU.add,
+                    )
         xb = {}
         for c, width in enumerate(CHUNKS):
             for s in range(2):
@@ -250,9 +252,6 @@ def tile_list_hank_pair_features_kernel(
                 if starts[c] < head:
                     xb[c, s] = scale_round_weave("V", "x%d_%d" % (c, s), th[s][:, :, cols], gain_sb, width)
                     continue
-                if starts[c] == head:
-                    for t in range(early, PACK):
-                        apply_gain(s, t)
                 xb[c, s] = sbuf("x%d_%d_bf" % (c, s), [P, PACK * width], BF16)
                 nc.scalar.copy(
                     out=woven(xb[c, s][:]), in_=planes(x_flat[s][:, :, starts[c] - head : starts[c] - head + width], width)

from contextlib import ExitStack

import concourse.mybir as mybir

K, T, S, H, NP, N = 1536, 2048, 1024, 512, 512, 384
FLOPS = 2 * (K * H * S + 2 * H * H * NP + H * N * NP)

F32 = mybir.dt.float32
BF16 = mybir.dt.bfloat16
I32 = mybir.dt.int32
U16 = mybir.dt.uint16
U8 = mybir.dt.uint8
FP8X4 = mybir.dt.float8_e4m3fn_x4
FP4X4 = mybir.dt.float4_e2m1fn_x4
ALU = mybir.AluOpType
ACT = mybir.ActivationFunctionType

P = 128
PACK = 4
PASSES = K // (P * PACK)
BANK = 512
FIRST_ROW = 32 - 4 * PASSES
CHUNKS = [128,128,128,128]
X_MODE = []
Z_MODE = ["S","S","V","V"]
LAST_PIECES = 2


def tile_list_hank_pair_features_kernel(
    tc, tab_words, tab_scales, offs, pos1, pos2, w1, b1, gain, w2_words, w2_scales, tone, w3_words, w3_scales, out
):
    nc = tc.nc
    with ExitStack() as ctx:
        keep = ctx.enter_context(tc.tile_pool(name="keep", bufs=1))
        psum = ctx.enter_context(tc.psum_pool(name="psum", bufs=8))

        def sbuf(name, shape, dtype):
            return keep.tile(shape, dtype, name=name, align_bytes=64)

        def bank(name):
            return psum.tile([P, BANK], F32, name=name, tag="bank")

        offs_sb = sbuf("offs_sb", [P, S // 16], U16)
        pos_sb = [sbuf("pos%d_sb" % s, [P, NP // 16], U16) for s in range(2)]
        tabw = [sbuf("tabw%d" % a, [P, T], U16) for a in range(PASSES)]
        tabs = sbuf("tabs", [P, T], U8)
        moved = sbuf("moved", [P, PASSES * S], U8)
        ws2 = sbuf("ws2", [P, H], U8)
        ws3 = sbuf("ws3", [P, N], U8)
        warm = sbuf("warm", [P, 1], F32)
        warm2 = sbuf("warm2", [P, 1], F32)

        nc.vector.memset(warm[:], 0.0)
        nc.scalar.activation(out=warm2[:], in_=warm[:], func=ACT.Tanh)
        for q in range(4):
            nc.vector.memset(tabs[32 * q : 32 * q + FIRST_ROW, :].bitcast(I32), 0)
        nc.gpsimd.memset(ws2[:].bitcast(I32), 0)
        nc.gpsimd.memset(ws3[:].bitcast(I32), 0)
        nc.gpsimd.memset(moved[:].bitcast(I32), 0)

        def w1_rows(a):
            return w1[a * P * PACK : (a + 1) * P * PACK, :].rearrange("(p j) c -> p j c", j=PACK)

        pieces = [1,2,2]
        w1_raw = [
            [sbuf("w1_raw%d_%d" % (a, u), [P, PACK, H // pieces[a]], F32) for u in range(pieces[a])]
            for a in range(PASSES)
        ]

        b1_sb = sbuf("b1_sb", [P, PACK], F32)
        gain_sb = sbuf("gain_sb", [P, PACK], F32)
        tone_sb = sbuf("tone_sb", [P, PACK], F32)
        nc.sync.dma_start(out=offs_sb[:], in_=offs)

        def load_table(a):
            nc.sync.dma_start(out=tabw[a][:].bitcast(I32), in_=tab_words[a].bitcast(I32))

        def load_w1(a, u):
            width = H // pieces[a]
            nc.sync.dma_start(out=w1_raw[a][u][:], in_=w1_rows(a)[:, :, u * width : (u + 1) * width])

        def load_table_scales():
            for q in range(4):
                nc.sync.dma_start(
                    out=tabs[32 * q + FIRST_ROW : 32 * (q + 1), :].bitcast(I32),
                    in_=tab_scales[:, 4 * q : 4 * q + 4, :].bitcast(I32),
                )

        load_table(0)
        load_w1(0, 0)
        load_table_scales()
        load_w1(1, 0)
        load_table(1)
        load_w1(1, 1)
        load_w1(2, 0)
        load_table(2)
        load_w1(2, 1)
        w2_raw = sbuf("w2_raw", [P, H], I32)
        w3_sb = sbuf("w3_sb", [P, 2 * N], U8)
        nc.sync.dma_start(out=b1_sb[:], in_=b1.rearrange("(p t) -> p t", t=PACK))
        nc.sync.dma_start(out=pos_sb[0][:], in_=pos1)
        nc.sync.dma_start(out=pos_sb[1][:], in_=pos2)

        picked_scales = sbuf("picked_scales", [P, S], U8)
        picked_words = [[sbuf("pw%d_%d" % (a, v), [P, BANK], U16) for v in range(2)] for a in range(PASSES)]

        def gather_words(a):
            for v in range(2):
                nc.vector.tensor_copy(
                    out=picked_words[a][v][:], in_=tabw[a][:].indirect(offs_sb[:, 32 * v : 32 * (v + 1)])
                )

        gather_words(0)
        nc.vector.tensor_copy(out=picked_scales[:], in_=tabs[:].indirect(offs_sb[:]))
        live = 3 * 32 + 4
        for a in range(PASSES):
            nc.sync.dma_start(
                out=moved[0:live, a * S : (a + 1) * S].bitcast(I32),
                in_=picked_scales[FIRST_ROW + 4 * a : FIRST_ROW + 4 * a + live, :].bitcast(I32),
            )
        nc.sync.dma_start(out=w2_raw[:], in_=w2_words[0].rearrange("p c i -> p (c i)").bitcast(I32))
        nc.sync.dma_start(out=gain_sb[:], in_=gain.rearrange("(p t) -> p t", t=PACK))
        for q in range(4):
            nc.sync.dma_start(
                out=ws2[32 * q : 32 * q + 4, :].bitcast(I32), in_=w2_scales[0, 4 * q : 4 * q + 4, :].bitcast(I32)
            )
        nc.sync.dma_start(out=tone_sb[:], in_=tone.rearrange("(p t) -> p t", t=PACK))
        nc.sync.dma_start(out=w3_sb[:].bitcast(I32), in_=w3_words[0].bitcast(I32))
        for q in range(4):
            nc.sync.dma_start(
                out=ws3[32 * q : 32 * q + 4, :].bitcast(I32), in_=w3_scales[0, 4 * q : 4 * q + 4, :].bitcast(I32)
            )


        def table_scales(a, v):
            return moved[:, a * S + v * BANK : a * S + (v + 1) * BANK]

        h_banks = [[bank("h_bank%d_%d" % (t, v)) for v in range(2)] for t in range(PACK)]
        w1_q = []
        for a in range(PASSES):
            grouped = sbuf("w1_grouped%d" % a, [P, PACK * H], BF16)
            by_m = grouped[:].rearrange("p (t m j) -> p m j t", t=PACK, j=PACK)
            m_width = P // pieces[a]
            for u in range(pieces[a]):
                nc.scalar.copy(
                    out=by_m[:, u * m_width : (u + 1) * m_width, :, :],
                    in_=w1_raw[a][u][:].rearrange("p j (m t) -> p m j t", t=PACK),
                )
            if a > 0:
                gather_words(a)
            codes = sbuf("w1_codes%d" % a, [P, H], I32)
            scales = sbuf("w1_scales%d" % a, [P, H], U8)
            cuts = [0, P, H] if a == PASSES - 1 else [0, H]
            if a == PASSES - 1:
                cuts = [0, P, 2 * P, H]
            for lo, hi in zip(cuts, cuts[1:]):
                nc.vector.quantize_mx(
                    out=codes[:, lo:hi].bitcast(FP8X4), scales=scales[:, lo:hi], in_=grouped[:, PACK * lo : PACK * hi]
                )
            w1_q.append((codes, scales))
        for t in range(PACK):
            for a in range(PASSES):
                codes, scales = w1_q[a]
                for v in range(2):
                    nc.tensor.matmul_mx(
                        out=h_banks[t][v][:],
                        lhsT=codes[:, t * P : (t + 1) * P].bitcast(FP8X4),
                        lhsT_scale=scales[:, t * P : (t + 1) * P],
                        rhs=picked_words[a][v][:].bitcast(FP4X4),
                        rhs_scale=table_scales(a, v),
                        start=(a == 0),
                        stop=(a == PASSES - 1),
                    )

        w2_codes = sbuf("w2_codes", [P, H], I32)
        w2_sc = sbuf("w2_sc", [P, H], U8)
        nc.vector.tensor_copy(
            out=w2_codes[:].rearrange("p (t m) -> p t m", t=PACK), in_=w2_raw[:].rearrange("p (m t) -> p t m", t=PACK)
        )
        nc.vector.tensor_copy(
            out=w2_sc[:].rearrange("p (t m) -> p t m", t=PACK), in_=ws2[:].rearrange("p (m t) -> p t m", t=PACK)
        )

        h = [sbuf("h%d" % t, [P, S], F32) for t in range(PACK)]
        for t in range(PACK):
            for v in range(2):
                cols = slice(v * BANK, (v + 1) * BANK)
                if t == 0 and v == 1:
                    nc.vector.tensor_scalar(
                        out=h[t][:, cols], in0=h_banks[t][v][:], scalar1=b1_sb[:, t : t + 1], scalar2=None, op0=ALU.add
                    )
                else:
                    nc.scalar.activation(
                        out=h[t][:, cols], in_=h_banks[t][v][:], func=ACT.Identity, bias=b1_sb[:, t : t + 1]
                    )

        def planes(ap, width):
            return ap.rearrange("p t (c i) -> p c t i", i=4)

        def woven(ap):
            return ap.rearrange("p (c i t) -> p c t i", t=PACK, i=4)

        def spread(vec, width):
            return vec[:].rearrange("p (a t b) -> p a t b", a=1, b=1).to_broadcast([P, width // 4, PACK, 4])

        def scale_round_weave(mode, name, src, vec, width):
            dst = sbuf(name + "_bf", [P, PACK * width], BF16)
            if mode == "V":
                nc.vector.tensor_tensor(out=woven(dst[:]), in0=planes(src, width), in1=spread(vec, width), op=ALU.mult)
            else:
                flat = sbuf(name + "_flat", [P, PACK, width], BF16)
                for t in range(PACK):
                    nc.scalar.activation(out=flat[:, t, :], in_=src[:, t, :], func=ACT.Copy, scale=vec[:, t : t + 1])
                if mode == "S":
                    nc.scalar.copy(out=woven(dst[:]), in_=planes(flat[:], width))
                else:
                    nc.vector.tensor_copy(out=woven(dst[:]), in_=planes(flat[:], width))
            return dst

        def quantize(name, src, width):
            codes = sbuf(name + "_codes", [P, width], I32)
            scales = sbuf(name + "_scales", [P, width], U8)
            nc.vector.quantize_mx(out=codes[:].bitcast(FP8X4), scales=scales[:], in_=src[:])
            return codes, scales

        starts = [sum(CHUNKS[:c]) for c in range(len(CHUNKS))]
        hg = [sbuf("hg%d" % s, [P, PACK, NP], F32) for s in range(2)]
        th = [sbuf("th%d" % s, [P, PACK, NP], F32) for s in range(2)]
        head = 128
        early = PACK
        x_flat = [sbuf("x_flat%d" % s, [P, PACK, NP - head], BF16) for s in range(2)]
        spans = [(t, 0, NP) for t in range(PACK - 1)] + [(PACK - 1, 0, head), (PACK - 1, head, NP)]
        for t, lo, hi in spans:
            for s in range(2):
                nc.vector.tensor_copy(out=hg[s][:, t, lo:hi], in_=h[t][:].indirect(pos_sb[s][:, lo // 16 : hi // 16]))
        for t, lo, hi in spans:
            for s in range(2):
                nc.scalar.activation(out=th[s][:, t, lo:hi], in_=hg[s][:, t, lo:hi], func=ACT.Tanh)
                if hi > head:
                    nc.gpsimd.tensor_scalar(
                        out=x_flat[s][:, t, :],
                        in0=th[s][:, t, head:],
                        scalar1=gain_sb[:, t : t + 1],
                        scalar2=0.0,
                        op0=ALU.mult,
                        op1=ALU.add,
                    )
        xb = {}
        for c, width in enumerate(CHUNKS):
            for s in range(2):
                cols = slice(starts[c], starts[c] + width)
                if starts[c] < head:
                    xb[c, s] = scale_round_weave("V", "x%d_%d" % (c, s), th[s][:, :, cols], gain_sb, width)
                    continue
                xb[c, s] = sbuf("x%d_%d_bf" % (c, s), [P, PACK * width], BF16)
                nc.scalar.copy(
                    out=woven(xb[c, s][:]), in_=planes(x_flat[s][:, :, starts[c] - head : starts[c] - head + width], width)
                )

        largers = []
        out_rows = out.rearrange("(g p) j -> p g j", p=P)
        for c, width in enumerate(CHUNKS):
            per_bank = BANK // width
            diff = []
            for s in range(2):
                codes, scales = quantize("xq%d_%d" % (c, s), xb[c, s], width)
                e = sbuf("e%d_%d" % (c, s), [P, PACK, width], F32)
                for t0 in range(0, PACK, per_bank):
                    f = bank("f%d_%d_%d" % (c, s, t0))
                    for t in range(t0, t0 + per_bank):
                        nc.tensor.matmul_mx(
                            out=f[:, (t - t0) * width : (t - t0 + 1) * width],
                            lhsT=w2_codes[:, t * P : (t + 1) * P].bitcast(FP8X4),
                            lhsT_scale=w2_sc[:, t * P : (t + 1) * P],
                            rhs=codes[:].bitcast(FP8X4),
                            rhs_scale=scales[:],
                            start=True,
                            stop=True,
                        )
                    nc.vector.tensor_tensor(
                        out=e[:, t0 : t0 + per_bank, :],
                        in0=hg[1 - s][:, t0 : t0 + per_bank, starts[c] : starts[c] + width],
                        in1=f[:].rearrange("p (t j) -> p t j", j=width),
                        op=ALU.subtract,
                    )
                diff.append(e)
            larger = sbuf("larger%d" % c, [P, PACK, width], F32)
            nc.vector.tensor_tensor(out=larger[:], in0=diff[0][:], in1=diff[1][:], op=ALU.max)
            largers.append(larger)
        for c, width in enumerate(CHUNKS):
            per_bank = BANK // width
            larger = largers[c]
            zb = scale_round_weave(Z_MODE[c], "z%d" % c, larger[:], tone_sb, width)
            codes, scales = quantize("zq%d" % c, zb, width)
            staged = sbuf("staged%d" % c, [P, N // P, width], F32)
            for g0 in range(0, N // P, per_bank):
                count = min(per_bank, N // P - g0)
                acc = bank("acc%d_%d" % (c, g0))
                for g in range(g0, g0 + count):
                    nc.tensor.matmul_mx(
                        out=acc[:, (g - g0) * width : (g - g0 + 1) * width],
                        lhsT=w3_sb[:, 2 * g * P : 2 * (g + 1) * P].bitcast(FP4X4),
                        lhsT_scale=ws3[:, g * P : (g + 1) * P],
                        rhs=codes[:].bitcast(FP8X4),
                        rhs_scale=scales[:],
                        start=True,
                        stop=True,
                    )
                nc.scalar.copy(
                    out=staged[:, g0 : g0 + count, :],
                    in_=acc[:, 0 : count * width].rearrange("p (g j) -> p g j", j=width),
                )
            nc.sync.dma_start(out=out_rows[:, :, starts[c] : starts[c] + width], in_=staged[:])
